import numpy as np
import ml_dtypes

BF16 = ml_dtypes.bfloat16


def bf(x):
    return np.asarray(x, np.float32).astype(BF16)


def f32(x):
    return np.asarray(x, np.float32)


def f64(x):
    return np.asarray(x).astype(np.float64)


def striped(idx):
    return np.tile(idx.reshape(-1, 16).T, (8, 1))


S, K, M, N, E, Q = 512, 256, 512, 512, 2, 256


def setup_inputs():
    return {"base": bf(np.random.standard_normal((M, S))), "x": bf(np.random.standard_normal((K, N))), "w": bf(np.random.standard_normal((E, K, M)) / np.sqrt(K)), "b": f32(0.5 * np.random.standard_normal((M, 1))), "offs": striped(np.random.permutation(S))}


def reference(base, x, w, b, offs):
    idx = offs[:16].T.reshape(-1)
    z = f64(base).copy()
    for e in range(E):
        z[:, idx[e * Q : (e + 1) * Q]] += f64(w)[e].T @ f64(x)[:, e * Q : (e + 1) * Q]
    return np.maximum(z + f64(b), 0.0)

@@ -1,0 +1,67 @@
+import concourse.mybir as mybir
+from concourse.masks import make_identity
+
+BF16, F32, U16 = mybir.dt.bfloat16, mybir.dt.float32, mybir.dt.uint16
+ADD, MAX = mybir.AluOpType.add, mybir.AluOpType.max
+RELU = mybir.ActivationFunctionType.Relu
+
+P = 128
+TOKENS = 512
+K, M, N = 256, 512, 512
+EXPERTS = 2
+PIECE = N // EXPERTS
+K_BLOCKS = K // P
+M_BLOCKS = M // P
+PIECE_COLS = PIECE // 16
+
+FLOPS = 2 * K * M * N
+
+
+def tile_scatter_matmul_kernel(tc, base, x, w, b, offs, out):
+    nc = tc.nc
+    with (
+        tc.tile_pool(name="held", bufs=1) as held,
+        tc.tile_pool(name="results", bufs=M_BLOCKS) as results,
+        tc.psum_pool(name="windows", bufs=1) as windows,
+    ):
+        offsets = held.tile([P, N // 16], U16, name="offsets")
+        nc.sync.dma_start(offsets[:], offs)
+
+        base_tiles = [held.tile([P, TOKENS], BF16, name=f"base{mb}") for mb in range(M_BLOCKS)]
+        for mb in range(M_BLOCKS):
+            queue = nc.sync if mb % 2 == 0 else nc.scalar
+            queue.dma_start(base_tiles[mb][:], base[mb * P : (mb + 1) * P, :])
+
+        w_tile = held.tile([P, EXPERTS * K_BLOCKS, M], BF16, name="w_tile")
+        nc.gpsimd.dma_start(w_tile[:], w.rearrange("e (kb p) m -> p (e kb) m", p=P))
+        x_tile = held.tile([P, K_BLOCKS, N], BF16, name="x_tile")
+        nc.sync.dma_start(x_tile[:], x.rearrange("(kb p) j -> p kb j", p=P))
+        bias = held.tile([P, M_BLOCKS], F32, name="bias")
+        nc.scalar.dma_start(bias[:], b.rearrange("(mb p) o -> p (mb o)", p=P))
+
+        identity = held.tile([P, P], BF16, name="identity")
+        make_identity(nc, identity[:])
+
+        window_tiles = [windows.tile([P, TOKENS], F32, name=f"window{mb}") for mb in range(M_BLOCKS)]
+        for mb in range(M_BLOCKS):
+            nc.tensor.matmul(window_tiles[mb][:], identity[:], base_tiles[mb][:], start=True, stop=False)
+
+        for mb in range(M_BLOCKS):
+            for e in range(EXPERTS):
+                piece = offsets[:, e * PIECE_COLS : (e + 1) * PIECE_COLS]
+                for kb in range(K_BLOCKS):
+                    last = e == EXPERTS - 1 and kb == K_BLOCKS - 1
+                    nc.tensor.matmul(
+                        window_tiles[mb][:].indirect(piece),
+                        w_tile[:, e * K_BLOCKS + kb, mb * P : (mb + 1) * P],
+                        x_tile[:, kb, e * PIECE : (e + 1) * PIECE],
+                        start=False,
+                        stop=last,
+                    )
+            result = results.tile([P, TOKENS], F32, name="result")
+            if mb % 2 == 0:
+                nc.scalar.activation(result[:], window_tiles[mb][:], RELU, bias=bias[:, mb : mb + 1])
+            else:
+                nc.vector.tensor_scalar(result[:], window_tiles[mb][:], bias[:, mb : mb + 1], 0.0, op0=ADD, op1=MAX)
+            queue = nc.sync if mb % 2 == 0 else nc.scalar
+            queue.dma_start(out[mb * P : (mb + 1) * P, :], result[:])

@@ -13,6 +13,9 @@ PIECE = N // EXPERTS
 K_BLOCKS = K // P
 M_BLOCKS = M // P
 PIECE_COLS = PIECE // 16
+WARM_UP = 2
+
+HALF = TOKENS // 2
 
 FLOPS = 2 * K * M * N
 
@@ -21,47 +24,62 @@ def tile_scatter_matmul_kernel(tc, base, x, w, b, offs, out):
     nc = tc.nc
     with (
         tc.tile_pool(name="held", bufs=1) as held,
-        tc.tile_pool(name="results", bufs=M_BLOCKS) as results,
+        tc.tile_pool(name="results", bufs=2 * M_BLOCKS) as results,
         tc.psum_pool(name="windows", bufs=1) as windows,
     ):
-        offsets = held.tile([P, N // 16], U16, name="offsets")
-        nc.sync.dma_start(offsets[:], offs)
-
         base_tiles = [held.tile([P, TOKENS], BF16, name=f"base{mb}") for mb in range(M_BLOCKS)]
-        for mb in range(M_BLOCKS):
-            queue = nc.sync if mb % 2 == 0 else nc.scalar
-            queue.dma_start(base_tiles[mb][:], base[mb * P : (mb + 1) * P, :])
-
-        w_tile = held.tile([P, EXPERTS * K_BLOCKS, M], BF16, name="w_tile")
-        nc.gpsimd.dma_start(w_tile[:], w.rearrange("e (kb p) m -> p (e kb) m", p=P))
-        x_tile = held.tile([P, K_BLOCKS, N], BF16, name="x_tile")
-        nc.sync.dma_start(x_tile[:], x.rearrange("(kb p) j -> p kb j", p=P))
+        x_tiles = [held.tile([P, N], BF16, name=f"x{kb}") for kb in range(K_BLOCKS)]
+        w_tiles = [[held.tile([P, M], BF16, name=f"w{e}{kb}") for kb in range(K_BLOCKS)] for e in range(EXPERTS)]
+        offsets = held.tile([P, N // 16], U16, name="offsets")
         bias = held.tile([P, M_BLOCKS], F32, name="bias")
+
+        queues = (nc.sync, nc.scalar)
+        for mb in range(M_BLOCKS):
+            queues[mb % 2].dma_start(base_tiles[mb][:], base[mb * P : (mb + 1) * P, :])
+        nc.sync.dma_start(offsets[:], offs)
+        for kb in range(K_BLOCKS):
+            nc.sync.dma_start(x_tiles[kb][:], x[kb * P : (kb + 1) * P, :])
+            nc.scalar.dma_start(w_tiles[0][kb][:], w[0, kb * P : (kb + 1) * P, :])
+        for e in range(1, EXPERTS):
+            for kb in range(K_BLOCKS):
+                queues[kb % 2].dma_start(w_tiles[e][kb][:], w[e, kb * P : (kb + 1) * P, :])
         nc.scalar.dma_start(bias[:], b.rearrange("(mb p) o -> p (mb o)", p=P))
+
+        zeros = held.tile([P, TOKENS], BF16, name="zeros")
+        nc.vector.memset(zeros[:], 0.0)
+        scratch = windows.tile([P, TOKENS], F32, name="scratch")
+        for _ in range(WARM_UP):
+            nc.tensor.matmul(scratch[:], zeros[:, :P], zeros[:], start=True, stop=True)
 
         identity = held.tile([P, P], BF16, name="identity")
         make_identity(nc, identity[:])
-
         window_tiles = [windows.tile([P, TOKENS], F32, name=f"window{mb}") for mb in range(M_BLOCKS)]
         for mb in range(M_BLOCKS):
             nc.tensor.matmul(window_tiles[mb][:], identity[:], base_tiles[mb][:], start=True, stop=False)
 
+        def scattered_matmul(e, kb, mb, stop):
+            nc.tensor.matmul(
+                window_tiles[mb][:].indirect(offsets[:, e * PIECE_COLS : (e + 1) * PIECE_COLS]),
+                w_tiles[e][kb][:, mb * P : (mb + 1) * P],
+                x_tiles[kb][:, e * PIECE : (e + 1) * PIECE],
+                start=False,
+                stop=stop,
+            )
+
+        for e in range(EXPERTS - 1):
+            for kb in range(K_BLOCKS):
+                for mb in range(M_BLOCKS):
+                    scattered_matmul(e, kb, mb, stop=False)
         for mb in range(M_BLOCKS):
-            for e in range(EXPERTS):
-                piece = offsets[:, e * PIECE_COLS : (e + 1) * PIECE_COLS]
-                for kb in range(K_BLOCKS):
-                    last = e == EXPERTS - 1 and kb == K_BLOCKS - 1
-                    nc.tensor.matmul(
-                        window_tiles[mb][:].indirect(piece),
-                        w_tile[:, e * K_BLOCKS + kb, mb * P : (mb + 1) * P],
-                        x_tile[:, kb, e * PIECE : (e + 1) * PIECE],
-                        start=False,
-                        stop=last,
+            for kb in range(K_BLOCKS):
+                scattered_matmul(EXPERTS - 1, kb, mb, stop=kb == K_BLOCKS - 1)
+            for half in range(2):
+                columns = slice(half * HALF, (half + 1) * HALF)
+                result = results.tile([P, HALF], F32, name="result")
+                if mb % 2 == 0:
+                    nc.scalar.activation(result[:], window_tiles[mb][:, columns], RELU, bias=bias[:, mb : mb + 1])
+                else:
+                    nc.vector.tensor_scalar(
+                        result[:], window_tiles[mb][:, columns], bias[:, mb : mb + 1], 0.0, op0=ADD, op1=MAX
                     )
-            result = results.tile([P, TOKENS], F32, name="result")
-            if mb % 2 == 0:
-                nc.scalar.activation(result[:], window_tiles[mb][:], RELU, bias=bias[:, mb : mb + 1])
-            else:
-                nc.vector.tensor_scalar(result[:], window_tiles[mb][:], bias[:, mb : mb + 1], 0.0, op0=ADD, op1=MAX)
-            queue = nc.sync if mb % 2 == 0 else nc.scalar
-            queue.dma_start(out[mb * P : (mb + 1) * P, :], result[:])
+                queues[half].dma_start(out[mb * P : (mb + 1) * P, columns], result[:])

@@ -66,13 +66,12 @@ def tile_scatter_matmul_kernel(tc, base, x, w, b, offs, out):
                 stop=stop,
             )
 
-        for e in range(EXPERTS - 1):
-            for kb in range(K_BLOCKS):
-                for mb in range(M_BLOCKS):
-                    scattered_matmul(e, kb, mb, stop=False)
+        steps = [(e, kb) for e in range(EXPERTS) for kb in range(K_BLOCKS)]
         for mb in range(M_BLOCKS):
-            for kb in range(K_BLOCKS):
-                scattered_matmul(EXPERTS - 1, kb, mb, stop=kb == K_BLOCKS - 1)
+            scattered_matmul(steps[0][0], steps[0][1], mb, stop=False)
+        for mb in range(M_BLOCKS):
+            for e, kb in steps[1:]:
+                scattered_matmul(e, kb, mb, stop=(e, kb) == steps[-1])
             for half in range(2):
                 columns = slice(half * HALF, (half + 1) * HALF)
                 result = results.tile([P, HALF], F32, name="result")

@@ -33,17 +33,16 @@ def tile_scatter_matmul_kernel(tc, base, x, w, b, offs, out):
         offsets = held.tile([P, N // 16], U16, name="offsets")
         bias = held.tile([P, M_BLOCKS], F32, name="bias")
 
-        queues = (nc.sync, nc.scalar)
         for mb in range(M_BLOCKS):
-            queues[mb % 2].dma_start(base_tiles[mb][:], base[mb * P : (mb + 1) * P, :])
+            nc.sync.dma_start(base_tiles[mb][:], base[mb * P : (mb + 1) * P, :])
         nc.sync.dma_start(offsets[:], offs)
         for kb in range(K_BLOCKS):
             nc.sync.dma_start(x_tiles[kb][:], x[kb * P : (kb + 1) * P, :])
-            nc.scalar.dma_start(w_tiles[0][kb][:], w[0, kb * P : (kb + 1) * P, :])
+            nc.sync.dma_start(w_tiles[0][kb][:], w[0, kb * P : (kb + 1) * P, :])
         for e in range(1, EXPERTS):
             for kb in range(K_BLOCKS):
-                queues[kb % 2].dma_start(w_tiles[e][kb][:], w[e, kb * P : (kb + 1) * P, :])
-        nc.scalar.dma_start(bias[:], b.rearrange("(mb p) o -> p (mb o)", p=P))
+                nc.sync.dma_start(w_tiles[e][kb][:], w[e, kb * P : (kb + 1) * P, :])
+        nc.sync.dma_start(bias[:], b.rearrange("(mb p) o -> p (mb o)", p=P))
 
         zeros = held.tile([P, TOKENS], BF16, name="zeros")
         nc.vector.memset(zeros[:], 0.0)
@@ -81,4 +80,4 @@ def tile_scatter_matmul_kernel(tc, base, x, w, b, offs, out):
                     nc.vector.tensor_scalar(
                         result[:], window_tiles[mb][:, columns], bias[:, mb : mb + 1], 0.0, op0=ADD, op1=MAX
                     )
-                queues[half].dma_start(out[mb * P : (mb + 1) * P, columns], result[:])
+                (nc.sync, nc.scalar)[half].dma_start(out[mb * P : (mb + 1) * P, columns], result[:])

@@ -15,8 +15,6 @@ M_BLOCKS = M // P
 PIECE_COLS = PIECE // 16
 WARM_UP = 2
 
-HALF = TOKENS // 2
-
 FLOPS = 2 * K * M * N
 
 
@@ -24,7 +22,7 @@ def tile_scatter_matmul_kernel(tc, base, x, w, b, offs, out):
     nc = tc.nc
     with (
         tc.tile_pool(name="held", bufs=1) as held,
-        tc.tile_pool(name="results", bufs=2 * M_BLOCKS) as results,
+        tc.tile_pool(name="results", bufs=M_BLOCKS) as results,
         tc.psum_pool(name="windows", bufs=1) as windows,
     ):
         base_tiles = [held.tile([P, TOKENS], BF16, name=f"base{mb}") for mb in range(M_BLOCKS)]
@@ -71,13 +69,9 @@ def tile_scatter_matmul_kernel(tc, base, x, w, b, offs, out):
         for mb in range(M_BLOCKS):
             for e, kb in steps[1:]:
                 scattered_matmul(e, kb, mb, stop=(e, kb) == steps[-1])
-            for half in range(2):
-                columns = slice(half * HALF, (half + 1) * HALF)
-                result = results.tile([P, HALF], F32, name="result")
-                if mb % 2 == 0:
-                    nc.scalar.activation(result[:], window_tiles[mb][:, columns], RELU, bias=bias[:, mb : mb + 1])
-                else:
-                    nc.vector.tensor_scalar(
-                        result[:], window_tiles[mb][:, columns], bias[:, mb : mb + 1], 0.0, op0=ADD, op1=MAX
-                    )
-                (nc.sync, nc.scalar)[half].dma_start(out[mb * P : (mb + 1) * P, columns], result[:])
+            result = results.tile([P, TOKENS], F32, name="result")
+            if mb % 2 == 0:
+                nc.scalar.activation(result[:], window_tiles[mb][:], RELU, bias=bias[:, mb : mb + 1])
+            else:
+                nc.vector.tensor_scalar(result[:], window_tiles[mb][:], bias[:, mb : mb + 1], 0.0, op0=ADD, op1=MAX)
+            nc.sync.dma_start(out[mb * P : (mb + 1) * P, :], result[:])

@@ -48,6 +48,9 @@ def tile_scatter_matmul_kernel(tc, base, x, w, b, offs, out):
         for _ in range(WARM_UP):
             nc.tensor.matmul(scratch[:], zeros[:, :P], zeros[:], start=True, stop=True)
 
+        early = held.tile([P, 1], F32, name="early")
+        nc.scalar.activation(early[:], zeros[:, 0:1], RELU)
+
         identity = held.tile([P, P], BF16, name="identity")
         make_identity(nc, identity[:])
         window_tiles = [windows.tile([P, TOKENS], F32, name=f"window{mb}") for mb in range(M_BLOCKS)]

import concourse.mybir as mybir
from concourse.masks import make_identity

BF16, F32, U16 = mybir.dt.bfloat16, mybir.dt.float32, mybir.dt.uint16
ADD, MAX = mybir.AluOpType.add, mybir.AluOpType.max
RELU = mybir.ActivationFunctionType.Relu

P = 128
TOKENS = 512
K, M, N = 256, 512, 512
EXPERTS = 2
PIECE = N // EXPERTS
K_BLOCKS = K // P
M_BLOCKS = M // P
PIECE_COLS = PIECE // 16
WARM_UP = 2

FLOPS = 2 * K * M * N


def tile_scatter_matmul_kernel(tc, base, x, w, b, offs, out):
    nc = tc.nc
    with (
        tc.tile_pool(name="held", bufs=1) as held,
        tc.tile_pool(name="results", bufs=M_BLOCKS) as results,
        tc.psum_pool(name="windows", bufs=1) as windows,
    ):
        base_tiles = [held.tile([P, TOKENS], BF16, name=f"base{mb}") for mb in range(M_BLOCKS)]
        x_tiles = [held.tile([P, N], BF16, name=f"x{kb}") for kb in range(K_BLOCKS)]
        w_tiles = [[held.tile([P, M], BF16, name=f"w{e}{kb}") for kb in range(K_BLOCKS)] for e in range(EXPERTS)]
        offsets = held.tile([P, N // 16], U16, name="offsets")
        bias = held.tile([P, M_BLOCKS], F32, name="bias")

        for mb in range(M_BLOCKS):
            nc.sync.dma_start(base_tiles[mb][:], base[mb * P : (mb + 1) * P, :])
        nc.sync.dma_start(offsets[:], offs)
        for kb in range(K_BLOCKS):
            nc.sync.dma_start(x_tiles[kb][:], x[kb * P : (kb + 1) * P, :])
            nc.sync.dma_start(w_tiles[0][kb][:], w[0, kb * P : (kb + 1) * P, :])
        for e in range(1, EXPERTS):
            for kb in range(K_BLOCKS):
                nc.sync.dma_start(w_tiles[e][kb][:], w[e, kb * P : (kb + 1) * P, :])
        nc.sync.dma_start(bias[:], b.rearrange("(mb p) o -> p (mb o)", p=P))

        zeros = held.tile([P, TOKENS], BF16, name="zeros")
        nc.vector.memset(zeros[:], 0.0)
        scratch = windows.tile([P, TOKENS], F32, name="scratch")
        for _ in range(WARM_UP):
            nc.tensor.matmul(scratch[:], zeros[:, :P], zeros[:], start=True, stop=True)

        early = held.tile([P, 1], F32, name="early")
        nc.scalar.activation(early[:], zeros[:, 0:1], RELU)

        identity = held.tile([P, P], BF16, name="identity")
        make_identity(nc, identity[:])
        window_tiles = [windows.tile([P, TOKENS], F32, name=f"window{mb}") for mb in range(M_BLOCKS)]
        for mb in range(M_BLOCKS):
            nc.tensor.matmul(window_tiles[mb][:], identity[:], base_tiles[mb][:], start=True, stop=False)

        def scattered_matmul(e, kb, mb, stop):
            nc.tensor.matmul(
                window_tiles[mb][:].indirect(offsets[:, e * PIECE_COLS : (e + 1) * PIECE_COLS]),
                w_tiles[e][kb][:, mb * P : (mb + 1) * P],
                x_tiles[kb][:, e * PIECE : (e + 1) * PIECE],
                start=False,
                stop=stop,
            )

        steps = [(e, kb) for e in range(EXPERTS) for kb in range(K_BLOCKS)]
        for mb in range(M_BLOCKS):
            scattered_matmul(steps[0][0], steps[0][1], mb, stop=False)
        for mb in range(M_BLOCKS):
            for e, kb in steps[1:]:
                scattered_matmul(e, kb, mb, stop=(e, kb) == steps[-1])
            result = results.tile([P, TOKENS], F32, name="result")
            if mb % 2 == 0:
                nc.scalar.activation(result[:], window_tiles[mb][:], RELU, bias=bias[:, mb : mb + 1])
            else:
                nc.vector.tensor_scalar(result[:], window_tiles[mb][:], bias[:, mb : mb + 1], 0.0, op0=ADD, op1=MAX)
            nc.sync.dma_start(out[mb * P : (mb + 1) * P, :], result[:])
